import numpy as np
import ml_dtypes


def mxq(x, axis, fmt="e4m3"):
    dtype, down = {"e4m3": (ml_dtypes.float8_e4m3fn, 7), "e5m2": (ml_dtypes.float8_e5m2, 14)}[fmt]
    v = np.moveaxis(np.asarray(x, np.float32).astype(ml_dtypes.bfloat16).astype(np.float64), axis, -1)
    blocks = v.reshape(v.shape[:-1] + (-1, 32))
    amax = np.abs(blocks).max(-1, keepdims=True)
    byte = np.maximum(np.where(amax > 0, np.frexp(amax)[1] - 1 + 127, 0) - down, 1)
    scale = np.exp2(byte - 127.0)
    codes = (blocks / scale).astype(np.float32).astype(dtype).astype(np.float64)
    return np.moveaxis((codes * scale).reshape(v.shape), -1, axis)


WIDE = False


def mx_kscale(k):
    if not WIDE:
        return np.ones(k)
    levels = np.array([10, -10, 5, -5, 0])
    if k % 512:
        return np.exp2(np.random.permutation(np.resize(levels, k // 32))).repeat(32)
    a = np.empty((k // 512, 16))
    for p in range(k // 512):
        a[p, :8] = np.random.permutation(np.resize(levels, 8))
        for g in range(8):
            far = levels[np.abs(levels - a[p, g]) >= 10]
            a[p, g + 8] = far[np.random.randint(len(far))]
    return np.exp2(a.ravel()).repeat(32)


def f64(x):
    return np.asarray(x).astype(np.float64)


def striped(idx):
    return np.tile(np.asarray(idx).reshape(-1, 16).T, (8, 1)).astype(np.uint16)


def unstriped(offs):
    return offs[:16].T.reshape(-1).astype(np.int64)


E2M1 = np.array([0.0, 0.5, 1.0, 1.5, 2.0, 3.0, 4.0, 6.0, -0.0, -0.5, -1.0, -1.5, -2.0, -3.0, -4.0, -6.0])


def pack_weight(w, fmt):
    k, n = w.shape
    w = f64(np.asarray(w, np.float32).astype(ml_dtypes.bfloat16)).reshape(k // 32, 32, n)
    amax = np.abs(w).max(1)
    if fmt == "e4m3":
        byte = np.frexp(amax)[1] - 1 + 127 - 7
    else:
        mant, ex = np.frexp(amax / 6.0)
        byte = np.where(mant > 0.5, ex, ex - 1) + 127
    byte = np.clip(np.where(amax > 0, byte, 1), 1, 254)
    scaled = (w * np.exp2(127.0 - byte)[:, None, :]).reshape(k, n).astype(np.float32)
    by_word = np.ascontiguousarray(scaled.reshape(k // 512, 128, 4, n).transpose(0, 1, 3, 2))
    if fmt == "e4m3":
        words = by_word.astype(ml_dtypes.float8_e4m3fn).view(np.uint8)
    else:
        c = by_word.astype(ml_dtypes.float4_e2m1fn).view(np.uint8) & 0xF
        words = (c[..., 0::2] | (c[..., 1::2] << 4)).reshape(k // 512, 128, 2 * n)
    return np.ascontiguousarray(words), np.ascontiguousarray(byte.astype(np.uint8).reshape(k // 512, 16, n))


def unpack_weight(words, scales, fmt):
    g, _, n = scales.shape
    words = np.ascontiguousarray(words).reshape(g, 128, n, -1)
    if fmt == "e4m3":
        vals = words.view(ml_dtypes.float8_e4m3fn).astype(np.float64)
    else:
        nib = np.empty((g, 128, n, 4), np.uint8)
        nib[..., 0::2] = words & 0xF
        nib[..., 1::2] = words >> 4
        vals = E2M1[nib]
    vals = vals * np.repeat(np.exp2(scales.astype(np.float64) - 127.0), 8, axis=1)[..., None]
    return vals.transpose(0, 1, 3, 2).reshape(g * 512, n)


def bf(x):
    return np.asarray(x, np.float32).astype(ml_dtypes.bfloat16)


def planes(Y):
    r, m = Y.shape
    b = f64(bf(Y)).reshape(r // 32, 32, m)
    amax = np.abs(b).max(1)
    byte = np.clip(np.where(amax > 0, np.frexp(amax)[1] - 1 + 127 - 7, 1), 1, 254)
    codes = (b * np.exp2(127.0 - byte)[:, None, :]).reshape(r, m).astype(np.float32).astype(ml_dtypes.float8_e4m3fn).view(np.uint8)
    words = codes.reshape(r // 512, 128, 4, m).transpose(0, 1, 3, 2)
    return np.ascontiguousarray(words), np.ascontiguousarray(byte.astype(np.uint8).reshape(r // 512, 16, m))


D, T, I, J, U, E = 512, 2048, 512, 512, 1024, 512


def setup_inputs():
    n = np.random.standard_normal
    idx = np.random.permutation(T)[:I]
    idx2 = np.random.permutation(U)[:J]
    idx3 = np.random.permutation(U)[:J]
    idx4 = np.random.permutation(U)[:J]
    fd = mx_kscale(D)
    fi = mx_kscale(I)
    ti = np.ones(T)
    ti[idx] = fi
    keysp = pack_weight(n((D, T)) / fd[:, None], "e2m1")
    return {
        "keys_words": keysp[0],
        "keys_scales": keysp[1],
        "notes": (n((D, U)) * 1.0 / np.sqrt(D) * fd[:, None]).astype(np.float32),
        "rowf": (np.random.uniform(0.02, 0.08, (I, 1)) * fi[:, None]).astype(np.float32),
        "vals": (n((E, T)) / ti).astype(np.float32),
        "mem": (np.random.uniform(0.3, 1.0, (1, J))).astype(np.float32),
        "offs": striped(idx),
        "offs2": striped(idx2),
        "offs3": striped(idx3),
        "offs4": striped(idx4),
    }


def reference(keys_words, keys_scales, notes, rowf, vals, mem, offs, offs2, offs3, offs4):
    idx = unstriped(offs)
    idx2 = unstriped(offs2)
    idx3 = unstriped(offs3)
    idx4 = unstriped(offs4)
    keysu = unpack_weight(keys_words, keys_scales, "e2m1")
    keysidxg = keysu[:, idx]
    notesq = mxq(f64(notes), 0, "e4m3")
    g1 = keysidxg.T @ notesq
    lo2 = np.minimum(g1[:, idx2], g1[:, idx3])
    hi2 = np.maximum(g1[:, idx2], g1[:, idx3])
    g0 = np.maximum(lo2, np.minimum(hi2, g1[:, idx4]))
    gr1 = g0 * f64(rowf)
    vt1 = f64(vals)[:, idx].T
    vt1q = mxq(vt1, 0, "e4m3")
    gr1q = mxq(gr1, 0, "e4m3")
    o = vt1q.T @ gr1q
    o1 = np.pad(o, ((0, 0), (1, 0)))[:, :J]
    y = o - o1 * f64(mem)
    words, scales = planes(y)
    return y, words, scales

@@ -1,0 +1,232 @@
+from contextlib import ExitStack
+
+import concourse.mybir as mybir
+from concourse.masks import make_identity
+
+D, T, I, J, U, E = 512, 2048, 512, 512, 1024, 512
+FLOPS = 2 * D * I * U + 2 * I * E * J
+
+F32 = mybir.dt.float32
+BF16 = mybir.dt.bfloat16
+I32 = mybir.dt.int32
+U32 = mybir.dt.uint32
+U16 = mybir.dt.uint16
+U8 = mybir.dt.uint8
+FP8X4 = mybir.dt.float8_e4m3fn_x4
+FP4X4 = mybir.dt.float4_e2m1fn_x4
+ALU = mybir.AluOpType
+COPY = mybir.ActivationFunctionType.Copy
+
+P = 128
+PACK = 4
+BANK = 512
+NOTE_CHUNKS = (256, 256, 256, 256)
+NOTE_ON_VECTOR = (3,)
+J_CHUNKS = (256, 128, 128)
+VECTOR_GATHERS = ((0, 0, 0), (0, 1, 0), (0, 2, 0), (0, 3, 0))
+VALS_ON_VECTOR = (1, 3)
+G1_ON_VECTOR = ((0, 2), (0, 3), (1, 1), (1, 3))
+Y_ON_VECTOR = (2,)
+
+
+def tile_attend_tab_middleof3_changes_pl_kernel(
+    tc, keys_words, keys_scales, notes, rowf, vals, mem, offs, offs2, offs3, offs4, out_0, out_1, out_2
+):
+    nc = tc.nc
+
+    def gather(on_vector, out, window, offsets):
+        if on_vector:
+            nc.vector.tensor_copy(out, window.indirect(offsets))
+        else:
+            nc.scalar.activation(out, window.indirect(offsets), COPY)
+
+    def move(on_vector, out, in_):
+        if on_vector:
+            nc.vector.tensor_copy(out, in_)
+        else:
+            nc.scalar.copy(out, in_)
+
+    def woven_out(t):
+        return t.rearrange("p (c i t) -> p c t i", i=4, t=PACK)
+
+    def woven_in(t):
+        return t.rearrange("p t (c i) -> p c t i", i=4)
+
+    with ExitStack() as ctx:
+        keep = ctx.enter_context(tc.tile_pool(name="keep", bufs=1))
+        psum = ctx.enter_context(tc.psum_pool(name="psum", bufs=8))
+
+        lists = [keep.tile([P, 32], U16, name=f"list{n}") for n in range(4)]
+        nc.sync.dma_start(lists[0][:], offs)
+        key_words = keep.tile([P, T], U16, name="key_words")
+        nc.sync.dma_start(key_words[:].bitcast(I32), keys_words[0].bitcast(I32))
+        key_scales = keep.tile([P, T], U8, name="key_scales")
+        nc.vector.memset(key_scales[:].bitcast(I32), 0)
+        for q in range(4):
+            nc.sync.dma_start(
+                key_scales[32 * q : 32 * q + 4, :].bitcast(I32), keys_scales[0, 4 * q : 4 * q + 4, :].bitcast(I32)
+            )
+        notes_view = notes.rearrange("(p t) u -> p t u", t=PACK)
+        note_raw = []
+        u0 = 0
+        for n, w in enumerate(NOTE_CHUNKS):
+            raw = keep.tile([P, PACK, w], F32, name=f"note_raw{n}")
+            nc.sync.dma_start(raw[:], notes_view[:, :, u0 : u0 + w])
+            note_raw.append((raw, u0, w))
+            u0 = u0 + w
+        for n, src in ((1, offs2), (2, offs3), (3, offs4)):
+            nc.sync.dma_start(lists[n][:], src)
+        vals_view = vals.rearrange("(p t) x -> p t x", t=PACK)
+        val_pool = [keep.tile([P, T], F32, name=f"val_pool{t}", tag=f"val_pool{t}") for t in range(PACK)]
+        for t in range(PACK):
+            nc.sync.dma_start(val_pool[t][:], vals_view[:, t, :])
+        factor = keep.tile([P, PACK], F32, name="factor")
+        nc.sync.dma_start(factor[:], rowf.rearrange("(p t) o -> p (t o)", t=PACK))
+        memory = keep.tile([P, J], F32, name="memory")
+        nc.sync.dma_start(memory[:], mem[0].partition_broadcast(P))
+        identity = keep.tile([P, P], F32, name="identity")
+        make_identity(nc, identity[:])
+
+        picked_words = keep.tile([P, I], U16, name="picked_words")
+        nc.vector.tensor_copy(picked_words[:], key_words[:].indirect(lists[0][:]))
+        dealt_scales = keep.tile([P, PACK, P], U8, name="dealt_scales", align_bytes=64)
+        nc.vector.tensor_copy(dealt_scales[:].rearrange("p t m -> p m t"), key_scales[:].indirect(lists[0][:]))
+        dealt_words = keep.tile([P, PACK, P], U16, name="dealt_words", align_bytes=64)
+        nc.vector.tensor_copy(dealt_words[:], picked_words[:].rearrange("p (m t) -> p t m", t=PACK))
+
+        note_codes = keep.tile([P, U], U32, name="note_codes", align_bytes=64)
+        note_scales = keep.tile([P, U], U8, name="note_scales", align_bytes=64)
+        wide = [keep.tile([P, U], F32, name=f"wide{t}") for t in range(PACK)]
+        for n, (raw, u0, w) in enumerate(note_raw):
+            woven = keep.tile([P, w * PACK], BF16, name=f"note_woven{n}", align_bytes=64)
+            move(n in NOTE_ON_VECTOR, woven_out(woven[:]), woven_in(raw[:]))
+            nc.vector.quantize_mx(note_codes[:, u0 : u0 + w].bitcast(FP8X4), note_scales[:, u0 : u0 + w], woven[:])
+            if (u0 + w) % BANK == 0:
+                cols = slice(u0 + w - BANK, u0 + w)
+                for t in range(PACK):
+                    acc = psum.tile([P, BANK], F32, name="bank", tag="bank")
+                    nc.tensor.matmul_mx(
+                        acc[:], dealt_words[:, t, :].bitcast(FP4X4), dealt_scales[:, t, :],
+                        note_codes[:, cols].bitcast(FP8X4), note_scales[:, cols], start=True, stop=True,
+                    )
+                    move((cols.start // BANK, t) in G1_ON_VECTOR, wide[t][:, cols], acc[:])
+
+        val_codes = keep.tile([P, E], U32, name="val_codes", align_bytes=64)
+        val_scales = keep.tile([P, E], U8, name="val_scales", align_bytes=64)
+        picked_vals = [keep.tile([P, I], BF16, name=f"picked_vals{t}", tag=f"picked_vals{t}") for t in range(PACK)]
+
+        def pick_values(t):
+            gather(t in VALS_ON_VECTOR, picked_vals[t][:], val_pool[t][:], lists[0][:])
+
+        def turn_values(pair):
+            bank = psum.tile([P, BANK], F32, name="bank", tag="bank")
+            turned = bank[:].rearrange("p (t u m) -> p t u m", t=2, u=2)
+            for s in range(2):
+                words = picked_vals[2 * pair + s][:].bitcast(F32)
+                for u in range(2):
+                    nc.tensor.transpose(turned[:, s, u, :], words[:, u : I // 2 : 2], identity[:])
+            woven = keep.tile([P, 2 * P * PACK], BF16, name=f"val_woven{pair}", tag=f"val_woven{pair}", align_bytes=64)
+            nc.scalar.copy(
+                woven[:].bitcast(F32).rearrange("p (t m u) -> p t m u", t=2, u=2), turned.rearrange("p t u m -> p t m u")
+            )
+            cols = slice(2 * P * pair, 2 * P * (pair + 1))
+            nc.vector.quantize_mx(val_codes[:, cols].bitcast(FP8X4), val_scales[:, cols], woven[:])
+
+        carried = keep.tile([P, PACK, J + 8], F32, name="carried")
+        nc.vector.memset(carried[:, :, 0:1], 0.0)
+        result = keep.tile([P, PACK, J], F32, name="result")
+        out_codes = keep.tile([P, J], U32, name="out_codes", align_bytes=64)
+        out_scales = keep.tile([P, J], U8, name="out_scales", align_bytes=64)
+        out_view = out_0.rearrange("(p t) j -> p t j", t=PACK)
+        code_view = out_1[0].rearrange("p j r -> p (j r)").bitcast(I32)
+        starts = [sum(J_CHUNKS[:c]) for c in range(len(J_CHUNKS))]
+        picks, middle, table, rounded = {}, {}, {}, {}
+
+        def pick(c, t0, nt, tag):
+            j0, w = starts[c], J_CHUNKS[c]
+            got = keep.tile([P, 3, nt, w], F32, name=f"picks{c}_{t0}", tag=tag)
+            picks[c, t0] = got
+            for s in range(nt):
+                t = t0 + s
+                for n in range(3):
+                    gather((c, t, n) in VECTOR_GATHERS, got[:, n, s, :], wide[t][:], lists[n + 1][:, j0 // 16 : (j0 + w) // 16])
+
+        def median(c, t0, nt, tag):
+            w = J_CHUNKS[c]
+            got = picks[c, t0]
+            if t0 == 0:
+                middle[c] = keep.tile([P, PACK, w], F32, name=f"middle{c}", tag=f"middle{c}")
+            work = keep.tile([P, 3, nt, w], F32, name=f"work{c}_{t0}", tag=tag)
+            nc.vector.tensor_tensor(work[:, 0], got[:, 0], got[:, 1], ALU.max)
+            nc.vector.tensor_tensor(work[:, 1], got[:, 0], got[:, 1], ALU.min)
+            nc.vector.tensor_tensor(work[:, 2], work[:, 0], got[:, 2], ALU.min)
+            nc.vector.tensor_tensor(middle[c][:, t0 : t0 + nt, :], work[:, 1], work[:, 2], ALU.max)
+
+        def close(c):
+            w = J_CHUNKS[c]
+            woven = keep.tile([P, w * PACK], BF16, name=f"table_woven{c}", align_bytes=64)
+            spread = factor[:].unsqueeze(1).unsqueeze(3).to_broadcast([P, w // 4, PACK, 4])
+            nc.vector.tensor_tensor(woven_out(woven[:]), woven_in(middle[c][:]), spread, ALU.mult)
+            codes = keep.tile([P, w], U32, name=f"table_codes{c}", align_bytes=64)
+            scales = keep.tile([P, w], U8, name=f"table_scales{c}", align_bytes=64)
+            nc.vector.quantize_mx(codes[:].bitcast(FP8X4), scales[:], woven[:])
+            table[c] = (codes, scales)
+
+        def product(c):
+            j0, w = starts[c], J_CHUNKS[c]
+            codes, scales = table[c]
+            per_bank = BANK // w
+            wc = w - 1 if j0 + w == J else w
+            for t0 in range(0, PACK, per_bank):
+                bank = psum.tile([P, BANK], F32, name="bank", tag="bank")
+                sums = bank[:].rearrange("p (s j) -> p s j", s=per_bank)
+                for s in range(per_bank):
+                    cols = slice(P * (t0 + s), P * (t0 + s + 1))
+                    nc.tensor.matmul_mx(
+                        sums[:, s, :], val_codes[:, cols].bitcast(FP8X4), val_scales[:, cols],
+                        codes[:].bitcast(FP8X4), scales[:], start=True, stop=True,
+                    )
+                rows = slice(t0, t0 + per_bank)
+                nc.vector.tensor_tensor(
+                    carried[:, rows, j0 + 1 : j0 + 1 + wc], sums[:, :, 0:wc],
+                    memory[:, j0 + 1 : j0 + 1 + wc].unsqueeze(1).to_broadcast([P, per_bank, wc]), ALU.mult,
+                )
+                nc.vector.tensor_tensor(result[:, rows, j0 : j0 + w], sums, carried[:, rows, j0 : j0 + w], ALU.subtract)
+            nc.sync.dma_start(out_view[:, :, j0 : j0 + w], result[:, :, j0 : j0 + w])
+            woven = keep.tile([P, w * PACK], BF16, name=f"out_woven{c}", align_bytes=64)
+            move(c in Y_ON_VECTOR, woven_out(woven[:]), woven_in(result[:, :, j0 : j0 + w]))
+            rounded[c] = woven
+
+        def planes(c):
+            j0, w = starts[c], J_CHUNKS[c]
+            nc.vector.quantize_mx(out_codes[:, j0 : j0 + w].bitcast(FP8X4), out_scales[:, j0 : j0 + w], rounded[c][:])
+            nc.sync.dma_start(code_view[:, j0 : j0 + w], out_codes[:, j0 : j0 + w].bitcast(I32))
+
+        pick(0, 0, 2, "picks_a")
+        pick(0, 2, 2, "picks_b")
+        pick_values(0)
+        pick_values(1)
+        turn_values(0)
+        median(0, 0, 2, "work_a")
+        pick_values(2)
+        pick_values(3)
+        turn_values(1)
+        median(0, 2, 2, "work_b")
+        close(0)
+        pick(1, 0, 4, "val_pool2")
+        product(0)
+        median(1, 0, 4, "work_b")
+        pick(2, 0, 2, "picks_b")
+        pick(2, 2, 2, "middle0")
+        close(1)
+        median(2, 0, 2, "work_b")
+        product(1)
+        median(2, 2, 2, "work_b")
+        close(2)
+        planes(0)
+        planes(1)
+        product(2)
+        planes(2)
+        for q in range(4):
+            eng = nc.sync if q % 2 == 0 else nc.scalar
+            eng.dma_start(out_2[0, 4 * q : 4 * q + 4, :].bitcast(I32), out_scales[32 * q : 32 * q + 4, :].bitcast(I32))

@@ -22,11 +22,12 @@ PACK = 4
 BANK = 512
 NOTE_CHUNKS = (256, 256, 256, 256)
 NOTE_ON_VECTOR = (3,)
+TURN_ON_VECTOR = ()
 J_CHUNKS = (256, 128, 128)
 VECTOR_GATHERS = ((0, 0, 0), (0, 1, 0), (0, 2, 0), (0, 3, 0))
-VALS_ON_VECTOR = (1, 3)
+VALS_ON_VECTOR = (1,)
 G1_ON_VECTOR = ((0, 2), (0, 3), (1, 1), (1, 3))
-Y_ON_VECTOR = (2,)
+Y_ON_VECTOR = (1, 2)
 
 
 def tile_attend_tab_middleof3_changes_pl_kernel(
@@ -57,13 +58,14 @@ def tile_attend_tab_middleof3_changes_pl_kernel(
         psum = ctx.enter_context(tc.psum_pool(name="psum", bufs=8))
 
         lists = [keep.tile([P, 32], U16, name=f"list{n}") for n in range(4)]
-        nc.sync.dma_start(lists[0][:], offs)
+        for n, src in enumerate((offs, offs2, offs3, offs4)):
+            nc.sync.dma_start(lists[n][:], src)
         key_words = keep.tile([P, T], U16, name="key_words")
         nc.sync.dma_start(key_words[:].bitcast(I32), keys_words[0].bitcast(I32))
         key_scales = keep.tile([P, T], U8, name="key_scales")
         nc.vector.memset(key_scales[:].bitcast(I32), 0)
         for q in range(4):
-            nc.sync.dma_start(
+            nc.scalar.dma_start(
                 key_scales[32 * q : 32 * q + 4, :].bitcast(I32), keys_scales[0, 4 * q : 4 * q + 4, :].bitcast(I32)
             )
         notes_view = notes.rearrange("(p t) u -> p t u", t=PACK)
@@ -74,10 +76,8 @@ def tile_attend_tab_middleof3_changes_pl_kernel(
             nc.sync.dma_start(raw[:], notes_view[:, :, u0 : u0 + w])
             note_raw.append((raw, u0, w))
             u0 = u0 + w
-        for n, src in ((1, offs2), (2, offs3), (3, offs4)):
-            nc.sync.dma_start(lists[n][:], src)
         vals_view = vals.rearrange("(p t) x -> p t x", t=PACK)
-        val_pool = [keep.tile([P, T], F32, name=f"val_pool{t}", tag=f"val_pool{t}") for t in range(PACK)]
+        val_pool = [keep.tile([P, T], F32, name=f"val_pool{t}", tag=f"val_pool{t}", align_bytes=64) for t in range(PACK)]
         for t in range(PACK):
             nc.sync.dma_start(val_pool[t][:], vals_view[:, t, :])
         factor = keep.tile([P, PACK], F32, name="factor")
@@ -113,39 +113,38 @@ def tile_attend_tab_middleof3_changes_pl_kernel(
 
         val_codes = keep.tile([P, E], U32, name="val_codes", align_bytes=64)
         val_scales = keep.tile([P, E], U8, name="val_scales", align_bytes=64)
-        picked_vals = [keep.tile([P, I], BF16, name=f"picked_vals{t}", tag=f"picked_vals{t}") for t in range(PACK)]
+        picked_vals = [keep.tile([P, I], BF16, name=f"picked_vals{t}", tag=f"picked_vals{t}", align_bytes=64) for t in range(PACK)]
 
         def pick_values(t):
             gather(t in VALS_ON_VECTOR, picked_vals[t][:], val_pool[t][:], lists[0][:])
 
-        def turn_values(pair):
+        def turn_values(pair, tag):
             bank = psum.tile([P, BANK], F32, name="bank", tag="bank")
             turned = bank[:].rearrange("p (t u m) -> p t u m", t=2, u=2)
             for s in range(2):
                 words = picked_vals[2 * pair + s][:].bitcast(F32)
                 for u in range(2):
                     nc.tensor.transpose(turned[:, s, u, :], words[:, u : I // 2 : 2], identity[:])
-            woven = keep.tile([P, 2 * P * PACK], BF16, name=f"val_woven{pair}", tag=f"val_woven{pair}", align_bytes=64)
-            nc.scalar.copy(
-                woven[:].bitcast(F32).rearrange("p (t m u) -> p t m u", t=2, u=2), turned.rearrange("p t u m -> p t m u")
+            woven = keep.tile([P, 2 * P * PACK], BF16, name=f"val_woven{pair}", tag=tag, align_bytes=64)
+            move(
+                pair in TURN_ON_VECTOR, woven[:].bitcast(F32).rearrange("p (t m u) -> p t m u", t=2, u=2), turned.rearrange("p t u m -> p t m u")
             )
             cols = slice(2 * P * pair, 2 * P * (pair + 1))
             nc.vector.quantize_mx(val_codes[:, cols].bitcast(FP8X4), val_scales[:, cols], woven[:])
 
         carried = keep.tile([P, PACK, J + 8], F32, name="carried")
         nc.vector.memset(carried[:, :, 0:1], 0.0)
-        result = keep.tile([P, PACK, J], F32, name="result")
-        out_codes = keep.tile([P, J], U32, name="out_codes", align_bytes=64)
         out_scales = keep.tile([P, J], U8, name="out_scales", align_bytes=64)
         out_view = out_0.rearrange("(p t) j -> p t j", t=PACK)
         code_view = out_1[0].rearrange("p j r -> p (j r)").bitcast(I32)
         starts = [sum(J_CHUNKS[:c]) for c in range(len(J_CHUNKS))]
-        picks, middle, table, rounded = {}, {}, {}, {}
+        picks, middle, table, rounded, results = {}, {}, {}, {}, {}
 
         def pick(c, t0, nt, tag):
             j0, w = starts[c], J_CHUNKS[c]
-            got = keep.tile([P, 3, nt, w], F32, name=f"picks{c}_{t0}", tag=tag)
-            picks[c, t0] = got
+            got = keep.tile([P, 3, nt, w], F32, name=f"picks{c}_{t0}", tag=tag, align_bytes=64)
+            for t in range(t0, t0 + nt):
+                picks[c, t] = (got, t - t0)
             for s in range(nt):
                 t = t0 + s
                 for n in range(3):
@@ -153,10 +152,11 @@ def tile_attend_tab_middleof3_changes_pl_kernel(
 
         def median(c, t0, nt, tag):
             w = J_CHUNKS[c]
-            got = picks[c, t0]
+            held, s0 = picks[c, t0]
+            got = held[:, :, s0 : s0 + nt, :]
             if t0 == 0:
-                middle[c] = keep.tile([P, PACK, w], F32, name=f"middle{c}", tag=f"middle{c}")
-            work = keep.tile([P, 3, nt, w], F32, name=f"work{c}_{t0}", tag=tag)
+                middle[c] = keep.tile([P, PACK, w], F32, name=f"middle{c}", tag=f"middle{c}", align_bytes=64)
+            work = keep.tile([P, 3, nt, w], F32, name=f"work{c}_{t0}", tag=tag, align_bytes=64)
             nc.vector.tensor_tensor(work[:, 0], got[:, 0], got[:, 1], ALU.max)
             nc.vector.tensor_tensor(work[:, 1], got[:, 0], got[:, 1], ALU.min)
             nc.vector.tensor_tensor(work[:, 2], work[:, 0], got[:, 2], ALU.min)
@@ -164,10 +164,10 @@ def tile_attend_tab_middleof3_changes_pl_kernel(
 
         def close(c):
             w = J_CHUNKS[c]
-            woven = keep.tile([P, w * PACK], BF16, name=f"table_woven{c}", align_bytes=64)
+            woven = keep.tile([P, w * PACK], BF16, name=f"table_woven{c}", tag=f"table_woven{c}", align_bytes=64)
             spread = factor[:].unsqueeze(1).unsqueeze(3).to_broadcast([P, w // 4, PACK, 4])
             nc.vector.tensor_tensor(woven_out(woven[:]), woven_in(middle[c][:]), spread, ALU.mult)
-            codes = keep.tile([P, w], U32, name=f"table_codes{c}", align_bytes=64)
+            codes = keep.tile([P, w], U32, name=f"table_codes{c}", tag=f"table_codes{c}", align_bytes=64)
             scales = keep.tile([P, w], U8, name=f"table_scales{c}", align_bytes=64)
             nc.vector.quantize_mx(codes[:].bitcast(FP8X4), scales[:], woven[:])
             table[c] = (codes, scales)
@@ -176,6 +176,8 @@ def tile_attend_tab_middleof3_changes_pl_kernel(
             j0, w = starts[c], J_CHUNKS[c]
             codes, scales = table[c]
             per_bank = BANK // w
+            result = keep.tile([P, PACK, w], F32, name=f"result{c}")
+            results[c] = result
             wc = w - 1 if j0 + w == J else w
             for t0 in range(0, PACK, per_bank):
                 bank = psum.tile([P, BANK], F32, name="bank", tag="bank")
@@ -191,42 +193,49 @@ def tile_attend_tab_middleof3_changes_pl_kernel(
                     carried[:, rows, j0 + 1 : j0 + 1 + wc], sums[:, :, 0:wc],
                     memory[:, j0 + 1 : j0 + 1 + wc].unsqueeze(1).to_broadcast([P, per_bank, wc]), ALU.mult,
                 )
-                nc.vector.tensor_tensor(result[:, rows, j0 : j0 + w], sums, carried[:, rows, j0 : j0 + w], ALU.subtract)
-            nc.sync.dma_start(out_view[:, :, j0 : j0 + w], result[:, :, j0 : j0 + w])
+                nc.vector.tensor_tensor(result[:, rows, :], sums, carried[:, rows, j0 : j0 + w], ALU.subtract)
+            nc.sync.dma_start(out_view[:, :, j0 : j0 + w], result[:])
+
+        def weave(c):
+            w = J_CHUNKS[c]
             woven = keep.tile([P, w * PACK], BF16, name=f"out_woven{c}", align_bytes=64)
-            move(c in Y_ON_VECTOR, woven_out(woven[:]), woven_in(result[:, :, j0 : j0 + w]))
+            move(c in Y_ON_VECTOR, woven_out(woven[:]), woven_in(results[c][:]))
             rounded[c] = woven
 
-        def planes(c):
+        def planes(c, tag):
             j0, w = starts[c], J_CHUNKS[c]
-            nc.vector.quantize_mx(out_codes[:, j0 : j0 + w].bitcast(FP8X4), out_scales[:, j0 : j0 + w], rounded[c][:])
-            nc.sync.dma_start(code_view[:, j0 : j0 + w], out_codes[:, j0 : j0 + w].bitcast(I32))
+            out_codes = keep.tile([P, w], U32, name=f"out_codes{c}", tag=tag, align_bytes=64)
+            nc.vector.quantize_mx(out_codes[:].bitcast(FP8X4), out_scales[:, j0 : j0 + w], rounded[c][:])
+            nc.sync.dma_start(code_view[:, j0 : j0 + w], out_codes[:].bitcast(I32))
 
         pick(0, 0, 2, "picks_a")
         pick(0, 2, 2, "picks_b")
         pick_values(0)
         pick_values(1)
-        turn_values(0)
         median(0, 0, 2, "work_a")
+        median(0, 2, 2, "work_b")
         pick_values(2)
         pick_values(3)
-        turn_values(1)
-        median(0, 2, 2, "work_b")
         close(0)
-        pick(1, 0, 4, "val_pool2")
+        turn_values(0, "val_woven0")
+        turn_values(1, "val_woven1")
+        pick(1, 0, 4, "val_pool3")
+        pick(2, 0, 4, "val_woven1")
         product(0)
-        median(1, 0, 4, "work_b")
-        pick(2, 0, 2, "picks_b")
-        pick(2, 2, 2, "middle0")
+        weave(0)
+        median(1, 0, 2, "table_woven0")
+        median(1, 2, 2, "table_codes0")
         close(1)
-        median(2, 0, 2, "work_b")
         product(1)
-        median(2, 2, 2, "work_b")
+        weave(1)
+        median(2, 0, 2, "table_woven1")
+        median(2, 2, 2, "table_codes1")
+        planes(1, "out_codes1")
         close(2)
-        planes(0)
-        planes(1)
+        planes(0, "table_woven2")
         product(2)
-        planes(2)
+        weave(2)
+        planes(2, "out_codes2")
         for q in range(4):
             eng = nc.sync if q % 2 == 0 else nc.scalar
             eng.dma_start(out_2[0, 4 * q : 4 * q + 4, :].bitcast(I32), out_scales[32 * q : 32 * q + 4, :].bitcast(I32))

@@ -22,12 +22,13 @@ PACK = 4
 BANK = 512
 NOTE_CHUNKS = (256, 256, 256, 256)
 NOTE_ON_VECTOR = (3,)
-TURN_ON_VECTOR = ()
+TURN_ON_VECTOR = (0, 1)
+PICK_CHUNKS = (256, 128, 128)
 J_CHUNKS = (256, 128, 128)
 VECTOR_GATHERS = ((0, 0, 0), (0, 1, 0), (0, 2, 0), (0, 3, 0))
 VALS_ON_VECTOR = (1,)
 G1_ON_VECTOR = ((0, 2), (0, 3), (1, 1), (1, 3))
-Y_ON_VECTOR = (1, 2)
+Y_ON_VECTOR = (2,)
 
 
 def tile_attend_tab_middleof3_changes_pl_kernel(
@@ -58,8 +59,7 @@ def tile_attend_tab_middleof3_changes_pl_kernel(
         psum = ctx.enter_context(tc.psum_pool(name="psum", bufs=8))
 
         lists = [keep.tile([P, 32], U16, name=f"list{n}") for n in range(4)]
-        for n, src in enumerate((offs, offs2, offs3, offs4)):
-            nc.sync.dma_start(lists[n][:], src)
+        nc.sync.dma_start(lists[0][:], offs)
         key_words = keep.tile([P, T], U16, name="key_words")
         nc.sync.dma_start(key_words[:].bitcast(I32), keys_words[0].bitcast(I32))
         key_scales = keep.tile([P, T], U8, name="key_scales")
@@ -76,6 +76,8 @@ def tile_attend_tab_middleof3_changes_pl_kernel(
             nc.sync.dma_start(raw[:], notes_view[:, :, u0 : u0 + w])
             note_raw.append((raw, u0, w))
             u0 = u0 + w
+        for n, src in ((1, offs2), (2, offs3), (3, offs4)):
+            nc.sync.dma_start(lists[n][:], src)
         vals_view = vals.rearrange("(p t) x -> p t x", t=PACK)
         val_pool = [keep.tile([P, T], F32, name=f"val_pool{t}", tag=f"val_pool{t}", align_bytes=64) for t in range(PACK)]
         for t in range(PACK):
@@ -97,25 +99,29 @@ def tile_attend_tab_middleof3_changes_pl_kernel(
         note_codes = keep.tile([P, U], U32, name="note_codes", align_bytes=64)
         note_scales = keep.tile([P, U], U8, name="note_scales", align_bytes=64)
         wide = [keep.tile([P, U], F32, name=f"wide{t}") for t in range(PACK)]
+        banks = {}
         for n, (raw, u0, w) in enumerate(note_raw):
             woven = keep.tile([P, w * PACK], BF16, name=f"note_woven{n}", align_bytes=64)
             move(n in NOTE_ON_VECTOR, woven_out(woven[:]), woven_in(raw[:]))
             nc.vector.quantize_mx(note_codes[:, u0 : u0 + w].bitcast(FP8X4), note_scales[:, u0 : u0 + w], woven[:])
-            if (u0 + w) % BANK == 0:
-                cols = slice(u0 + w - BANK, u0 + w)
-                for t in range(PACK):
-                    acc = psum.tile([P, BANK], F32, name="bank", tag="bank")
-                    nc.tensor.matmul_mx(
-                        acc[:], dealt_words[:, t, :].bitcast(FP4X4), dealt_scales[:, t, :],
-                        note_codes[:, cols].bitcast(FP8X4), note_scales[:, cols], start=True, stop=True,
-                    )
-                    move((cols.start // BANK, t) in G1_ON_VECTOR, wide[t][:, cols], acc[:])
+        for n, (raw, u0, w) in enumerate(note_raw):
+            half, at = divmod(u0, BANK)
+            for t in range(PACK):
+                if at == 0:
+                    banks[t] = psum.tile([P, BANK], F32, name="bank", tag="bank")
+                nc.tensor.matmul_mx(
+                    banks[t][:, at : at + w], dealt_words[:, t, :].bitcast(FP4X4), dealt_scales[:, t, :],
+                    note_codes[:, u0 : u0 + w].bitcast(FP8X4), note_scales[:, u0 : u0 + w], start=True, stop=True,
+                )
+                if at + w == BANK:
+                    move((half, t) in G1_ON_VECTOR, wide[t][:, half * BANK : (half + 1) * BANK], banks[t][:])
 
         val_codes = keep.tile([P, E], U32, name="val_codes", align_bytes=64)
         val_scales = keep.tile([P, E], U8, name="val_scales", align_bytes=64)
-        picked_vals = [keep.tile([P, I], BF16, name=f"picked_vals{t}", tag=f"picked_vals{t}", align_bytes=64) for t in range(PACK)]
+        picked_vals = {}
 
-        def pick_values(t):
+        def pick_values(t, tag):
+            picked_vals[t] = keep.tile([P, I], BF16, name=f"picked_vals{t}", tag=tag, align_bytes=64)
             gather(t in VALS_ON_VECTOR, picked_vals[t][:], val_pool[t][:], lists[0][:])
 
         def turn_values(pair, tag):
@@ -132,16 +138,15 @@ def tile_attend_tab_middleof3_changes_pl_kernel(
             cols = slice(2 * P * pair, 2 * P * (pair + 1))
             nc.vector.quantize_mx(val_codes[:, cols].bitcast(FP8X4), val_scales[:, cols], woven[:])
 
-        carried = keep.tile([P, PACK, J + 8], F32, name="carried")
-        nc.vector.memset(carried[:, :, 0:1], 0.0)
         out_scales = keep.tile([P, J], U8, name="out_scales", align_bytes=64)
         out_view = out_0.rearrange("(p t) j -> p t j", t=PACK)
         code_view = out_1[0].rearrange("p j r -> p (j r)").bitcast(I32)
         starts = [sum(J_CHUNKS[:c]) for c in range(len(J_CHUNKS))]
+        pick_starts = [sum(PICK_CHUNKS[:c]) for c in range(len(PICK_CHUNKS))]
         picks, middle, table, rounded, results = {}, {}, {}, {}, {}
 
         def pick(c, t0, nt, tag):
-            j0, w = starts[c], J_CHUNKS[c]
+            j0, w = pick_starts[c], PICK_CHUNKS[c]
             got = keep.tile([P, 3, nt, w], F32, name=f"picks{c}_{t0}", tag=tag, align_bytes=64)
             for t in range(t0, t0 + nt):
                 picks[c, t] = (got, t - t0)
@@ -151,7 +156,7 @@ def tile_attend_tab_middleof3_changes_pl_kernel(
                     gather((c, t, n) in VECTOR_GATHERS, got[:, n, s, :], wide[t][:], lists[n + 1][:, j0 // 16 : (j0 + w) // 16])
 
         def median(c, t0, nt, tag):
-            w = J_CHUNKS[c]
+            w = PICK_CHUNKS[c]
             held, s0 = picks[c, t0]
             got = held[:, :, s0 : s0 + nt, :]
             if t0 == 0:
@@ -164,19 +169,24 @@ def tile_attend_tab_middleof3_changes_pl_kernel(
 
         def close(c):
             w = J_CHUNKS[c]
+            home = max(n for n, at in enumerate(pick_starts) if at <= starts[c])
+            first = starts[c] - pick_starts[home]
             woven = keep.tile([P, w * PACK], BF16, name=f"table_woven{c}", tag=f"table_woven{c}", align_bytes=64)
             spread = factor[:].unsqueeze(1).unsqueeze(3).to_broadcast([P, w // 4, PACK, 4])
-            nc.vector.tensor_tensor(woven_out(woven[:]), woven_in(middle[c][:]), spread, ALU.mult)
+            nc.vector.tensor_tensor(woven_out(woven[:]), woven_in(middle[home][:, :, first : first + w]), spread, ALU.mult)
             codes = keep.tile([P, w], U32, name=f"table_codes{c}", tag=f"table_codes{c}", align_bytes=64)
             scales = keep.tile([P, w], U8, name=f"table_scales{c}", align_bytes=64)
             nc.vector.quantize_mx(codes[:].bitcast(FP8X4), scales[:], woven[:])
             table[c] = (codes, scales)
 
-        def product(c):
+        carried = keep.tile([P, PACK, J + 8], F32, name="carried")
+        nc.vector.memset(carried[:, :, 0:1], 0.0)
+
+        def product(c, tag):
             j0, w = starts[c], J_CHUNKS[c]
             codes, scales = table[c]
             per_bank = BANK // w
-            result = keep.tile([P, PACK, w], F32, name=f"result{c}")
+            result = keep.tile([P, PACK, w], F32, name=f"result{c}", tag=tag, align_bytes=64)
             results[c] = result
             wc = w - 1 if j0 + w == J else w
             for t0 in range(0, PACK, per_bank):
@@ -210,31 +220,31 @@ def tile_attend_tab_middleof3_changes_pl_kernel(
 
         pick(0, 0, 2, "picks_a")
         pick(0, 2, 2, "picks_b")
-        pick_values(0)
-        pick_values(1)
+        pick_values(1, "pv1")
         median(0, 0, 2, "work_a")
         median(0, 2, 2, "work_b")
-        pick_values(2)
-        pick_values(3)
+        pick_values(0, "pv0")
+        pick_values(2, "pv2")
+        pick_values(3, "pv3")
         close(0)
         turn_values(0, "val_woven0")
         turn_values(1, "val_woven1")
         pick(1, 0, 4, "val_pool3")
         pick(2, 0, 4, "val_woven1")
-        product(0)
+        product(0, "result0")
         weave(0)
         median(1, 0, 2, "table_woven0")
         median(1, 2, 2, "table_codes0")
         close(1)
-        product(1)
-        weave(1)
-        median(2, 0, 2, "table_woven1")
-        median(2, 2, 2, "table_codes1")
-        planes(1, "out_codes1")
+        median(2, 0, 2, "table_woven0")
+        median(2, 2, 2, "table_woven1")
         close(2)
-        planes(0, "table_woven2")
-        product(2)
+        product(1, "result1")
+        product(2, "result2")
+        weave(1)
         weave(2)
+        planes(0, "table_woven2")
+        planes(1, "out_codes1")
         planes(2, "out_codes2")
         for q in range(4):
             eng = nc.sync if q % 2 == 0 else nc.scalar

@@ -22,11 +22,11 @@ PACK = 4
 BANK = 512
 NOTE_CHUNKS = (256, 256, 256, 256)
 NOTE_ON_VECTOR = (3,)
-TURN_ON_VECTOR = (0, 1)
-PICK_CHUNKS = (256, 128, 128)
+TURN_ON_VECTOR = (1,)
+PICK_CHUNKS = (384, 128)
 J_CHUNKS = (256, 128, 128)
 VECTOR_GATHERS = ((0, 0, 0), (0, 1, 0), (0, 2, 0), (0, 3, 0))
-VALS_ON_VECTOR = (1,)
+VALS_ON_VECTOR = ()
 G1_ON_VECTOR = ((0, 2), (0, 3), (1, 1), (1, 3))
 Y_ON_VECTOR = (2,)
 
@@ -116,7 +116,9 @@ def tile_attend_tab_middleof3_changes_pl_kernel(
                 if at + w == BANK:
                     move((half, t) in G1_ON_VECTOR, wide[t][:, half * BANK : (half + 1) * BANK], banks[t][:])
 
-        val_codes = keep.tile([P, E], U32, name="val_codes", align_bytes=64)
+        val_woven = {}
+        table_woven = {}
+        val_tiles = {}
         val_scales = keep.tile([P, E], U8, name="val_scales", align_bytes=64)
         picked_vals = {}
 
@@ -135,8 +137,13 @@ def tile_attend_tab_middleof3_changes_pl_kernel(
             move(
                 pair in TURN_ON_VECTOR, woven[:].bitcast(F32).rearrange("p (t m u) -> p t m u", t=2, u=2), turned.rearrange("p t u m -> p t m u")
             )
+            val_woven[pair] = woven
+
+        def quantise_values(pair, tag):
+            codes = keep.tile([P, 2 * P], U32, name=f"val_codes{pair}", tag=tag, align_bytes=64)
+            val_tiles[pair] = codes
             cols = slice(2 * P * pair, 2 * P * (pair + 1))
-            nc.vector.quantize_mx(val_codes[:, cols].bitcast(FP8X4), val_scales[:, cols], woven[:])
+            nc.vector.quantize_mx(codes[:].bitcast(FP8X4), val_scales[:, cols], val_woven[pair][:])
 
         out_scales = keep.tile([P, J], U8, name="out_scales", align_bytes=64)
         out_view = out_0.rearrange("(p t) j -> p t j", t=PACK)
@@ -150,9 +157,9 @@ def tile_attend_tab_middleof3_changes_pl_kernel(
             got = keep.tile([P, 3, nt, w], F32, name=f"picks{c}_{t0}", tag=tag, align_bytes=64)
             for t in range(t0, t0 + nt):
                 picks[c, t] = (got, t - t0)
-            for s in range(nt):
+            for s, n in sorted(((s, n) for s in range(nt) for n in range(3)), key=lambda sn: (sn[0] // 2, sn[1], sn[0])):
                 t = t0 + s
-                for n in range(3):
+                if True:
                     gather((c, t, n) in VECTOR_GATHERS, got[:, n, s, :], wide[t][:], lists[n + 1][:, j0 // 16 : (j0 + w) // 16])
 
         def median(c, t0, nt, tag):
@@ -174,9 +181,13 @@ def tile_attend_tab_middleof3_changes_pl_kernel(
             woven = keep.tile([P, w * PACK], BF16, name=f"table_woven{c}", tag=f"table_woven{c}", align_bytes=64)
             spread = factor[:].unsqueeze(1).unsqueeze(3).to_broadcast([P, w // 4, PACK, 4])
             nc.vector.tensor_tensor(woven_out(woven[:]), woven_in(middle[home][:, :, first : first + w]), spread, ALU.mult)
-            codes = keep.tile([P, w], U32, name=f"table_codes{c}", tag=f"table_codes{c}", align_bytes=64)
+            table_woven[c] = woven
+
+        def quantise_table(c, tag):
+            w = J_CHUNKS[c]
+            codes = keep.tile([P, w], U32, name=f"table_codes{c}", tag=tag, align_bytes=64)
             scales = keep.tile([P, w], U8, name=f"table_scales{c}", align_bytes=64)
-            nc.vector.quantize_mx(codes[:].bitcast(FP8X4), scales[:], woven[:])
+            nc.vector.quantize_mx(codes[:].bitcast(FP8X4), scales[:], table_woven[c][:])
             table[c] = (codes, scales)
 
         carried = keep.tile([P, PACK, J + 8], F32, name="carried")
@@ -195,7 +206,7 @@ def tile_attend_tab_middleof3_changes_pl_kernel(
                 for s in range(per_bank):
                     cols = slice(P * (t0 + s), P * (t0 + s + 1))
                     nc.tensor.matmul_mx(
-                        sums[:, s, :], val_codes[:, cols].bitcast(FP8X4), val_scales[:, cols],
+                        sums[:, s, :], val_tiles[(t0 + s) // 2][:, P * ((t0 + s) % 2) : P * ((t0 + s) % 2 + 1)].bitcast(FP8X4), val_scales[:, cols],
                         codes[:].bitcast(FP8X4), scales[:], start=True, stop=True,
                     )
                 rows = slice(t0, t0 + per_bank)
@@ -220,30 +231,32 @@ def tile_attend_tab_middleof3_changes_pl_kernel(
 
         pick(0, 0, 2, "picks_a")
         pick(0, 2, 2, "picks_b")
-        pick_values(1, "pv1")
         median(0, 0, 2, "work_a")
         median(0, 2, 2, "work_b")
         pick_values(0, "pv0")
-        pick_values(2, "pv2")
-        pick_values(3, "pv3")
-        close(0)
+        pick_values(1, "pv1")
         turn_values(0, "val_woven0")
-        turn_values(1, "val_woven1")
+        pick_values(2, "pv2")
+        pick_values(3, "pv1")
+        close(0)
+        quantise_table(0, "table_codes0")
+        quantise_values(0, "work_b")
+        close(1)
+        turn_values(1, "table_woven0")
+        quantise_values(1, "vc1")
         pick(1, 0, 4, "val_pool3")
-        pick(2, 0, 4, "val_woven1")
         product(0, "result0")
         weave(0)
         median(1, 0, 2, "table_woven0")
         median(1, 2, 2, "table_codes0")
-        close(1)
-        median(2, 0, 2, "table_woven0")
-        median(2, 2, 2, "table_woven1")
+        quantise_table(1, "table_codes0")
         close(2)
+        quantise_table(2, "table_codes2")
         product(1, "result1")
         product(2, "result2")
         weave(1)
         weave(2)
-        planes(0, "table_woven2")
+        planes(0, "table_woven1")
         planes(1, "out_codes1")
         planes(2, "out_codes2")
         for q in range(4):

from contextlib import ExitStack

import concourse.mybir as mybir
from concourse.masks import make_identity

D, T, I, J, U, E = 512, 2048, 512, 512, 1024, 512
FLOPS = 2 * D * I * U + 2 * I * E * J

F32 = mybir.dt.float32
BF16 = mybir.dt.bfloat16
I32 = mybir.dt.int32
U32 = mybir.dt.uint32
U16 = mybir.dt.uint16
U8 = mybir.dt.uint8
FP8X4 = mybir.dt.float8_e4m3fn_x4
FP4X4 = mybir.dt.float4_e2m1fn_x4
ALU = mybir.AluOpType
COPY = mybir.ActivationFunctionType.Copy

P = 128
PACK = 4
BANK = 512
NOTE_CHUNKS = (256, 256, 256, 256)
NOTE_ON_VECTOR = (3,)
TURN_ON_VECTOR = (1,)
PICK_CHUNKS = (384, 128)
J_CHUNKS = (256, 128, 128)
VECTOR_GATHERS = ((0, 0, 0), (0, 1, 0), (0, 2, 0), (0, 3, 0))
VALS_ON_VECTOR = ()
G1_ON_VECTOR = ((0, 2), (0, 3), (1, 1), (1, 3))
Y_ON_VECTOR = (2,)


def tile_attend_tab_middleof3_changes_pl_kernel(
    tc, keys_words, keys_scales, notes, rowf, vals, mem, offs, offs2, offs3, offs4, out_0, out_1, out_2
):
    nc = tc.nc

    def gather(on_vector, out, window, offsets):
        if on_vector:
            nc.vector.tensor_copy(out, window.indirect(offsets))
        else:
            nc.scalar.activation(out, window.indirect(offsets), COPY)

    def move(on_vector, out, in_):
        if on_vector:
            nc.vector.tensor_copy(out, in_)
        else:
            nc.scalar.copy(out, in_)

    def woven_out(t):
        return t.rearrange("p (c i t) -> p c t i", i=4, t=PACK)

    def woven_in(t):
        return t.rearrange("p t (c i) -> p c t i", i=4)

    with ExitStack() as ctx:
        keep = ctx.enter_context(tc.tile_pool(name="keep", bufs=1))
        psum = ctx.enter_context(tc.psum_pool(name="psum", bufs=8))

        lists = [keep.tile([P, 32], U16, name=f"list{n}") for n in range(4)]
        nc.sync.dma_start(lists[0][:], offs)
        key_words = keep.tile([P, T], U16, name="key_words")
        nc.sync.dma_start(key_words[:].bitcast(I32), keys_words[0].bitcast(I32))
        key_scales = keep.tile([P, T], U8, name="key_scales")
        nc.vector.memset(key_scales[:].bitcast(I32), 0)
        for q in range(4):
            nc.scalar.dma_start(
                key_scales[32 * q : 32 * q + 4, :].bitcast(I32), keys_scales[0, 4 * q : 4 * q + 4, :].bitcast(I32)
            )
        notes_view = notes.rearrange("(p t) u -> p t u", t=PACK)
        note_raw = []
        u0 = 0
        for n, w in enumerate(NOTE_CHUNKS):
            raw = keep.tile([P, PACK, w], F32, name=f"note_raw{n}")
            nc.sync.dma_start(raw[:], notes_view[:, :, u0 : u0 + w])
            note_raw.append((raw, u0, w))
            u0 = u0 + w
        for n, src in ((1, offs2), (2, offs3), (3, offs4)):
            nc.sync.dma_start(lists[n][:], src)
        vals_view = vals.rearrange("(p t) x -> p t x", t=PACK)
        val_pool = [keep.tile([P, T], F32, name=f"val_pool{t}", tag=f"val_pool{t}", align_bytes=64) for t in range(PACK)]
        for t in range(PACK):
            nc.sync.dma_start(val_pool[t][:], vals_view[:, t, :])
        factor = keep.tile([P, PACK], F32, name="factor")
        nc.sync.dma_start(factor[:], rowf.rearrange("(p t) o -> p (t o)", t=PACK))
        memory = keep.tile([P, J], F32, name="memory")
        nc.sync.dma_start(memory[:], mem[0].partition_broadcast(P))
        identity = keep.tile([P, P], F32, name="identity")
        make_identity(nc, identity[:])

        picked_words = keep.tile([P, I], U16, name="picked_words")
        nc.vector.tensor_copy(picked_words[:], key_words[:].indirect(lists[0][:]))
        dealt_scales = keep.tile([P, PACK, P], U8, name="dealt_scales", align_bytes=64)
        nc.vector.tensor_copy(dealt_scales[:].rearrange("p t m -> p m t"), key_scales[:].indirect(lists[0][:]))
        dealt_words = keep.tile([P, PACK, P], U16, name="dealt_words", align_bytes=64)
        nc.vector.tensor_copy(dealt_words[:], picked_words[:].rearrange("p (m t) -> p t m", t=PACK))

        note_codes = keep.tile([P, U], U32, name="note_codes", align_bytes=64)
        note_scales = keep.tile([P, U], U8, name="note_scales", align_bytes=64)
        wide = [keep.tile([P, U], F32, name=f"wide{t}") for t in range(PACK)]
        banks = {}
        for n, (raw, u0, w) in enumerate(note_raw):
            woven = keep.tile([P, w * PACK], BF16, name=f"note_woven{n}", align_bytes=64)
            move(n in NOTE_ON_VECTOR, woven_out(woven[:]), woven_in(raw[:]))
            nc.vector.quantize_mx(note_codes[:, u0 : u0 + w].bitcast(FP8X4), note_scales[:, u0 : u0 + w], woven[:])
        for n, (raw, u0, w) in enumerate(note_raw):
            half, at = divmod(u0, BANK)
            for t in range(PACK):
                if at == 0:
                    banks[t] = psum.tile([P, BANK], F32, name="bank", tag="bank")
                nc.tensor.matmul_mx(
                    banks[t][:, at : at + w], dealt_words[:, t, :].bitcast(FP4X4), dealt_scales[:, t, :],
                    note_codes[:, u0 : u0 + w].bitcast(FP8X4), note_scales[:, u0 : u0 + w], start=True, stop=True,
                )
                if at + w == BANK:
                    move((half, t) in G1_ON_VECTOR, wide[t][:, half * BANK : (half + 1) * BANK], banks[t][:])

        val_woven = {}
        table_woven = {}
        val_tiles = {}
        val_scales = keep.tile([P, E], U8, name="val_scales", align_bytes=64)
        picked_vals = {}

        def pick_values(t, tag):
            picked_vals[t] = keep.tile([P, I], BF16, name=f"picked_vals{t}", tag=tag, align_bytes=64)
            gather(t in VALS_ON_VECTOR, picked_vals[t][:], val_pool[t][:], lists[0][:])

        def turn_values(pair, tag):
            bank = psum.tile([P, BANK], F32, name="bank", tag="bank")
            turned = bank[:].rearrange("p (t u m) -> p t u m", t=2, u=2)
            for s in range(2):
                words = picked_vals[2 * pair + s][:].bitcast(F32)
                for u in range(2):
                    nc.tensor.transpose(turned[:, s, u, :], words[:, u : I // 2 : 2], identity[:])
            woven = keep.tile([P, 2 * P * PACK], BF16, name=f"val_woven{pair}", tag=tag, align_bytes=64)
            move(
                pair in TURN_ON_VECTOR, woven[:].bitcast(F32).rearrange("p (t m u) -> p t m u", t=2, u=2), turned.rearrange("p t u m -> p t m u")
            )
            val_woven[pair] = woven

        def quantise_values(pair, tag):
            codes = keep.tile([P, 2 * P], U32, name=f"val_codes{pair}", tag=tag, align_bytes=64)
            val_tiles[pair] = codes
            cols = slice(2 * P * pair, 2 * P * (pair + 1))
            nc.vector.quantize_mx(codes[:].bitcast(FP8X4), val_scales[:, cols], val_woven[pair][:])

        out_scales = keep.tile([P, J], U8, name="out_scales", align_bytes=64)
        out_view = out_0.rearrange("(p t) j -> p t j", t=PACK)
        code_view = out_1[0].rearrange("p j r -> p (j r)").bitcast(I32)
        starts = [sum(J_CHUNKS[:c]) for c in range(len(J_CHUNKS))]
        pick_starts = [sum(PICK_CHUNKS[:c]) for c in range(len(PICK_CHUNKS))]
        picks, middle, table, rounded, results = {}, {}, {}, {}, {}

        def pick(c, t0, nt, tag):
            j0, w = pick_starts[c], PICK_CHUNKS[c]
            got = keep.tile([P, 3, nt, w], F32, name=f"picks{c}_{t0}", tag=tag, align_bytes=64)
            for t in range(t0, t0 + nt):
                picks[c, t] = (got, t - t0)
            for s, n in sorted(((s, n) for s in range(nt) for n in range(3)), key=lambda sn: (sn[0] // 2, sn[1], sn[0])):
                t = t0 + s
                if True:
                    gather((c, t, n) in VECTOR_GATHERS, got[:, n, s, :], wide[t][:], lists[n + 1][:, j0 // 16 : (j0 + w) // 16])

        def median(c, t0, nt, tag):
            w = PICK_CHUNKS[c]
            held, s0 = picks[c, t0]
            got = held[:, :, s0 : s0 + nt, :]
            if t0 == 0:
                middle[c] = keep.tile([P, PACK, w], F32, name=f"middle{c}", tag=f"middle{c}", align_bytes=64)
            work = keep.tile([P, 3, nt, w], F32, name=f"work{c}_{t0}", tag=tag, align_bytes=64)
            nc.vector.tensor_tensor(work[:, 0], got[:, 0], got[:, 1], ALU.max)
            nc.vector.tensor_tensor(work[:, 1], got[:, 0], got[:, 1], ALU.min)
            nc.vector.tensor_tensor(work[:, 2], work[:, 0], got[:, 2], ALU.min)
            nc.vector.tensor_tensor(middle[c][:, t0 : t0 + nt, :], work[:, 1], work[:, 2], ALU.max)

        def close(c):
            w = J_CHUNKS[c]
            home = max(n for n, at in enumerate(pick_starts) if at <= starts[c])
            first = starts[c] - pick_starts[home]
            woven = keep.tile([P, w * PACK], BF16, name=f"table_woven{c}", tag=f"table_woven{c}", align_bytes=64)
            spread = factor[:].unsqueeze(1).unsqueeze(3).to_broadcast([P, w // 4, PACK, 4])
            nc.vector.tensor_tensor(woven_out(woven[:]), woven_in(middle[home][:, :, first : first + w]), spread, ALU.mult)
            table_woven[c] = woven

        def quantise_table(c, tag):
            w = J_CHUNKS[c]
            codes = keep.tile([P, w], U32, name=f"table_codes{c}", tag=tag, align_bytes=64)
            scales = keep.tile([P, w], U8, name=f"table_scales{c}", align_bytes=64)
            nc.vector.quantize_mx(codes[:].bitcast(FP8X4), scales[:], table_woven[c][:])
            table[c] = (codes, scales)

        carried = keep.tile([P, PACK, J + 8], F32, name="carried")
        nc.vector.memset(carried[:, :, 0:1], 0.0)

        def product(c, tag):
            j0, w = starts[c], J_CHUNKS[c]
            codes, scales = table[c]
            per_bank = BANK // w
            result = keep.tile([P, PACK, w], F32, name=f"result{c}", tag=tag, align_bytes=64)
            results[c] = result
            wc = w - 1 if j0 + w == J else w
            for t0 in range(0, PACK, per_bank):
                bank = psum.tile([P, BANK], F32, name="bank", tag="bank")
                sums = bank[:].rearrange("p (s j) -> p s j", s=per_bank)
                for s in range(per_bank):
                    cols = slice(P * (t0 + s), P * (t0 + s + 1))
                    nc.tensor.matmul_mx(
                        sums[:, s, :], val_tiles[(t0 + s) // 2][:, P * ((t0 + s) % 2) : P * ((t0 + s) % 2 + 1)].bitcast(FP8X4), val_scales[:, cols],
                        codes[:].bitcast(FP8X4), scales[:], start=True, stop=True,
                    )
                rows = slice(t0, t0 + per_bank)
                nc.vector.tensor_tensor(
                    carried[:, rows, j0 + 1 : j0 + 1 + wc], sums[:, :, 0:wc],
                    memory[:, j0 + 1 : j0 + 1 + wc].unsqueeze(1).to_broadcast([P, per_bank, wc]), ALU.mult,
                )
                nc.vector.tensor_tensor(result[:, rows, :], sums, carried[:, rows, j0 : j0 + w], ALU.subtract)
            nc.sync.dma_start(out_view[:, :, j0 : j0 + w], result[:])

        def weave(c):
            w = J_CHUNKS[c]
            woven = keep.tile([P, w * PACK], BF16, name=f"out_woven{c}", align_bytes=64)
            move(c in Y_ON_VECTOR, woven_out(woven[:]), woven_in(results[c][:]))
            rounded[c] = woven

        def planes(c, tag):
            j0, w = starts[c], J_CHUNKS[c]
            out_codes = keep.tile([P, w], U32, name=f"out_codes{c}", tag=tag, align_bytes=64)
            nc.vector.quantize_mx(out_codes[:].bitcast(FP8X4), out_scales[:, j0 : j0 + w], rounded[c][:])
            nc.sync.dma_start(code_view[:, j0 : j0 + w], out_codes[:].bitcast(I32))

        pick(0, 0, 2, "picks_a")
        pick(0, 2, 2, "picks_b")
        median(0, 0, 2, "work_a")
        median(0, 2, 2, "work_b")
        pick_values(0, "pv0")
        pick_values(1, "pv1")
        turn_values(0, "val_woven0")
        pick_values(2, "pv2")
        pick_values(3, "pv1")
        close(0)
        quantise_table(0, "table_codes0")
        quantise_values(0, "work_b")
        close(1)
        turn_values(1, "table_woven0")
        quantise_values(1, "vc1")
        pick(1, 0, 4, "val_pool3")
        product(0, "result0")
        weave(0)
        median(1, 0, 2, "table_woven0")
        median(1, 2, 2, "table_codes0")
        quantise_table(1, "table_codes0")
        close(2)
        quantise_table(2, "table_codes2")
        product(1, "result1")
        product(2, "result2")
        weave(1)
        weave(2)
        planes(0, "table_woven1")
        planes(1, "out_codes1")
        planes(2, "out_codes2")
        for q in range(4):
            eng = nc.sync if q % 2 == 0 else nc.scalar
            eng.dma_start(out_2[0, 4 * q : 4 * q + 4, :].bitcast(I32), out_scales[32 * q : 32 * q + 4, :].bitcast(I32))
